import numpy as np
import ml_dtypes


def mxq(x, axis, fmt="e4m3"):
    dtype, down = {"e4m3": (ml_dtypes.float8_e4m3fn, 7), "e5m2": (ml_dtypes.float8_e5m2, 14)}[fmt]
    v = np.moveaxis(np.asarray(x, np.float32).astype(ml_dtypes.bfloat16).astype(np.float64), axis, -1)
    blocks = v.reshape(v.shape[:-1] + (-1, 32))
    amax = np.abs(blocks).max(-1, keepdims=True)
    byte = np.maximum(np.where(amax > 0, np.frexp(amax)[1] - 1 + 127, 0) - down, 1)
    scale = np.exp2(byte - 127.0)
    codes = (blocks / scale).astype(np.float32).astype(dtype).astype(np.float64)
    return np.moveaxis((codes * scale).reshape(v.shape), -1, axis)


WIDE = False


def mx_kscale(k):
    if not WIDE:
        return np.ones(k)
    levels = np.array([24, -24, 12, -12, 0])
    if k % 512:
        return np.exp2(np.random.permutation(np.resize(levels, k // 32))).repeat(32)
    a = np.empty((k // 512, 16))
    for p in range(k // 512):
        a[p, :8] = np.random.permutation(np.resize(levels, 8))
        for g in range(8):
            far = levels[np.abs(levels - a[p, g]) >= 10]
            a[p, g + 8] = far[np.random.randint(len(far))]
    return np.exp2(a.ravel()).repeat(32)


def f64(x):
    return np.asarray(x).astype(np.float64)


def striped(idx):
    return np.tile(idx.reshape(-1, 16).T, (8, 1)).astype(np.uint16)


def unstriped(offs):
    return offs[:16].T.reshape(-1).astype(np.int64)


E2M1 = np.array([0.0, 0.5, 1.0, 1.5, 2.0, 3.0, 4.0, 6.0, -0.0, -0.5, -1.0, -1.5, -2.0, -3.0, -4.0, -6.0])


def pack_weight(w, fmt):
    k, n = w.shape
    w = f64(np.asarray(w, np.float32).astype(ml_dtypes.bfloat16)).reshape(k // 32, 32, n)
    amax = np.abs(w).max(1)
    if fmt == "e4m3":
        byte = np.frexp(amax)[1] - 1 + 127 - 7
    else:
        mant, ex = np.frexp(amax / 6.0)
        byte = np.where(mant > 0.5, ex, ex - 1) + 127
    byte = np.clip(np.where(amax > 0, byte, 1), 1, 254)
    scaled = (w * np.exp2(127.0 - byte)[:, None, :]).reshape(k, n).astype(np.float32)
    by_word = np.ascontiguousarray(scaled.reshape(k // 512, 128, 4, n).transpose(0, 1, 3, 2))
    if fmt == "e4m3":
        words = by_word.astype(ml_dtypes.float8_e4m3fn).view(np.uint8)
    else:
        c = by_word.astype(ml_dtypes.float4_e2m1fn).view(np.uint8) & 0xF
        words = (c[..., 0::2] | (c[..., 1::2] << 4)).reshape(k // 512, 128, 2 * n)
    return np.ascontiguousarray(words), np.ascontiguousarray(byte.astype(np.uint8).reshape(k // 512, 16, n))


def unpack_weight(words, scales, fmt):
    g, _, n = scales.shape
    words = np.ascontiguousarray(words).reshape(g, 128, n, -1)
    if fmt == "e4m3":
        vals = words.view(ml_dtypes.float8_e4m3fn).astype(np.float64)
    else:
        nib = np.empty((g, 128, n, 4), np.uint8)
        nib[..., 0::2] = words & 0xF
        nib[..., 1::2] = words >> 4
        vals = E2M1[nib]
    vals = vals * np.repeat(np.exp2(scales.astype(np.float64) - 127.0), 8, axis=1)[..., None]
    return vals.transpose(0, 1, 3, 2).reshape(g * 512, n)


def sigm(f):
    return 1.0 / (1.0 + np.exp(-np.maximum(f, -700.0)))


K, N, T, J = 512, 512, 2048, 1024


def setup_inputs():
    n = np.random.standard_normal
    s = mx_kscale(K)[:, None]
    p_tab = pack_weight(n((K, T)) * s, "e4m3")
    p_wb = pack_weight(n((K, N)) / np.sqrt(2 * K) / s, "e4m3")
    p_wc = pack_weight(n((K, N)) / np.sqrt(K) / s, "e4m3")
    return {
        "tab_words": p_tab[0],
        "tab_scales": p_tab[1],
        "wa": (n((K, N)) / np.sqrt(2 * K) / s).astype(np.float32),
        "wb_words": p_wb[0],
        "wb_scales": p_wb[1],
        "wc_words": p_wc[0],
        "wc_scales": p_wc[1],
        "wo": (n((K, N)) / np.sqrt(K) / s).astype(np.float32),
        "wgo": np.tile(np.random.uniform(0.5, 2.0, J), (128, 1)).astype(np.float32),
        "offs": striped(np.random.permutation(T)[:J]),
        "offs2": striped(np.random.permutation(T)[:J]),
    }


def reference(tab_words, tab_scales, wa, wb_words, wb_scales, wc_words, wc_scales, wo, wgo, offs, offs2):
    idx = unstriped(offs)
    idx2 = unstriped(offs2)
    tab_ = unpack_weight(tab_words, tab_scales, "e4m3")[:, idx]
    tabb_ = unpack_weight(tab_words, tab_scales, "e4m3")[:, idx2]
    wa_ = mxq(f64(wa), 0, "e4m3")
    wb_ = unpack_weight(wb_words, wb_scales, "e4m3")
    za = wa_.T @ tabb_ + wb_.T @ tab_
    eta = sigm(za)
    wc_ = unpack_weight(wc_words, wc_scales, "e4m3")
    ms = wc_.T @ tab_
    wo_ = mxq(f64(wo), 0, "e4m3")
    ow = wo_.T @ tabb_
    out = np.zeros((N, T))
    out[:, idx2] = f64(wgo)[0] * (ow + eta * ms)
    return out

@@ -1,0 +1,195 @@
+from contextlib import ExitStack
+
+import concourse.mybir as mybir
+from concourse.masks import make_identity
+
+K, N, T, J = 512, 512, 2048, 1024
+FLOPS = 4 * 2 * K * N * J
+
+F32 = mybir.dt.float32
+BF16 = mybir.dt.bfloat16
+I32 = mybir.dt.int32
+U32 = mybir.dt.uint32
+U16 = mybir.dt.uint16
+U8 = mybir.dt.uint8
+FP8X4 = mybir.dt.float8_e4m3fn_x4
+MULT = mybir.AluOpType.mult
+SIGMOID = mybir.ActivationFunctionType.Sigmoid
+COPY = mybir.ActivationFunctionType.Copy
+
+P = 128
+PACK = 4
+PER_COLUMN = 16
+EDGE_TILES = J // P
+ROW_TILES = N // P
+GATHER_CUTS = (0, 256, 512, 1024)
+SCATTER_CUTS = ((0, 2, 6, 8), (0, 3, 6, 8), (0, 4, 8), (0, 5, 8))
+
+
+def load_scale_rows(queue, plane, scales):
+    for q in range(4):
+        queue.dma_start(
+            out=plane[32 * q : 32 * q + 4, :].bitcast(I32),
+            in_=scales[0, 4 * q : 4 * q + 4, :].bitcast(I32),
+        )
+
+
+def words_of(packed):
+    return packed[0].rearrange("p c i -> p (c i)").bitcast(I32)
+
+
+def tile_list_rgg_own_kernel(
+    tc, tab_words, tab_scales, wa, wb_words, wb_scales, wc_words, wc_scales, wo, wgo, offs, offs2, out
+):
+    nc = tc.nc
+    with ExitStack() as ctx:
+        keep = ctx.enter_context(tc.tile_pool(name="keep", bufs=1))
+        landing = ctx.enter_context(tc.tile_pool(name="landing", bufs=1))
+        ring = ctx.enter_context(tc.tile_pool(name="ring", bufs=3))
+        psum = ctx.enter_context(tc.psum_pool(name="psum", bufs=2))
+
+        src_list = keep.tile([P, J // PER_COLUMN], U16, name="src_list")
+        dst_list = keep.tile([P, J // PER_COLUMN], U16, name="dst_list")
+        nc.sync.dma_start(dst_list[:], offs2)
+        nc.sync.dma_start(src_list[:], offs)
+
+        tab_plane = keep.tile([P, T], U8, name="tab_plane", align_bytes=64)
+        nc.gpsimd.memset(tab_plane[:].bitcast(I32), 0)
+        load_scale_rows(nc.sync, tab_plane, tab_scales)
+
+        edge_rows = keep.tile([P, P], F32, name="edge_rows")
+        nc.vector.memset(edge_rows[:], 0.0)
+        nc.sync.dma_start(out=edge_rows[0:EDGE_TILES, :], in_=wgo[0].rearrange("(c m) -> c m", m=P))
+
+        draft = landing.tile([P, 7168], F32, name="draft", offset=0, align_bytes=64)
+        make_identity(nc, draft[:, 0:P])
+        ident = keep.tile([P, P], F32, name="ident")
+        nc.gpsimd.tensor_copy(ident[:], draft[:, 0:P])
+
+        planes = {}
+        for name in ("wb", "wc"):
+            planes[name] = keep.tile([P, N], U8, name=name + "_plane", align_bytes=64)
+            nc.gpsimd.memset(planes[name][:].bitcast(I32), 0)
+        load_scale_rows(nc.gpsimd, planes["wc"], wc_scales)
+
+        raw = {}
+        for name, w, at in (("wa", wa, 0), ("wo", wo, 8192)):
+            raw[name] = landing.tile([P, PACK, N], F32, name=name + "_raw", offset=at, align_bytes=64)
+            nc.sync.dma_start(out=raw[name][:], in_=w.rearrange("(p i) n -> p i n", i=PACK))
+
+        table = landing.tile([P, T], I32, name="table", offset=16384, align_bytes=64)
+        nc.sync.dma_start(out=table[:], in_=words_of(tab_words))
+        load_scale_rows(nc.sync, planes["wb"], wb_scales)
+        codes = {}
+        for name, packed, at in (("wb", wb_words, 24576), ("wc", wc_words, 26624)):
+            codes[name] = landing.tile([P, N], I32, name=name + "_codes", offset=at, align_bytes=64)
+            nc.sync.dma_start(out=codes[name][:], in_=words_of(packed))
+
+        pages = [keep.tile([P, T], F32, name="page%d" % r) for r in range(ROW_TILES)]
+        for r in range(2):
+            nc.vector.memset(pages[r][:], 0.0)
+
+        for r in range(2, ROW_TILES):
+            for half in range(2):
+                nc.gpsimd.memset(pages[r][:, half * J : (half + 1) * J], 0.0)
+
+        picked_scales = {}
+        for name, lst in (("dst", dst_list), ("src", src_list)):
+            picked_scales[name] = keep.tile([P, J], U8, name=name + "_scales", align_bytes=64)
+            nc.vector.tensor_copy(picked_scales[name][:], tab_plane[:].indirect(lst[:]))
+
+        def quantise(name):
+            grouped = keep.tile([P, N, PACK], BF16, name=name + "_grouped", align_bytes=64)
+            nc.scalar.copy(
+                out=grouped[:].rearrange("p (c m) i -> p c i m", m=4),
+                in_=raw[name][:].rearrange("p i (c m) -> p c i m", m=4),
+            )
+            codes[name] = keep.tile([P, N], U32, name=name + "_codes", align_bytes=64)
+            planes[name] = keep.tile([P, N], U8, name=name + "_plane", align_bytes=64)
+            nc.vector.quantize_mx(
+                out=codes[name][:].bitcast(FP8X4),
+                scales=planes[name][:],
+                in_=grouped[:].rearrange("p n i -> p (n i)"),
+            )
+
+        picked_words = {}
+
+        def gather_words(g):
+            lo, hi = GATHER_CUTS[g], GATHER_CUTS[g + 1]
+            for name, lst in (("dst", dst_list), ("src", src_list)):
+                words = keep.tile([P, hi - lo], U32, name="%s_words%d" % (name, g), align_bytes=64)
+                nc.vector.tensor_copy(
+                    words[:], table[:].bitcast(U32).indirect(lst[:, lo // PER_COLUMN : hi // PER_COLUMN])
+                )
+                for e in range(lo // P, hi // P):
+                    picked_words[name, e] = words[:, e * P - lo : (e + 1) * P - lo]
+
+        quantise("wa")
+        gather_words(0)
+        quantise("wo")
+        for g in range(1, len(GATHER_CUTS) - 1):
+            gather_words(g)
+
+        turned = psum.tile([P, ROW_TILES, P], F32, name="turned")
+        nc.tensor.transpose(turned[:, 0, :], edge_rows[:], ident[:])
+        edge_weight = keep.tile([P, EDGE_TILES], F32, name="edge_weight")
+        nc.scalar.copy(out=edge_weight[:], in_=turned[:, 0, 0:EDGE_TILES])
+
+        def product(acc, side, e, weight, start, stop):
+            nc.tensor.matmul_mx(
+                out=acc[:],
+                lhsT=picked_words[side, e].bitcast(FP8X4),
+                lhsT_scale=picked_scales[side][:, e * P : (e + 1) * P],
+                rhs=codes[weight][:].bitcast(FP8X4),
+                rhs_scale=planes[weight][:],
+                start=start,
+                stop=stop,
+            )
+
+        def edge_tile_front(e):
+            za = psum.tile([P, N], F32, name="za")
+            ms = psum.tile([P, N], F32, name="ms")
+            ow = psum.tile([P, N], F32, name="ow")
+            product(za, "dst", e, "wa", True, False)
+            product(za, "src", e, "wb", False, True)
+            product(ms, "src", e, "wc", True, True)
+            product(ow, "dst", e, "wo", True, True)
+            eta = ring.tile([P, N], F32, name="eta")
+            nc.scalar.activation(out=eta[:], in_=za[:], func=SIGMOID)
+            gated = ring.tile([P, N], F32, name="gated")
+            msg = ring.tile([P, N], F32, name="msg")
+            nc.scalar.activation(out=msg[:], in_=ms[:], func=COPY, scale=edge_weight[:, e : e + 1])
+            nc.gpsimd.tensor_tensor(out=gated[:], in0=msg[:], in1=eta[:], op=MULT)
+            own = ring.tile([P, N], F32, name="own")
+            nc.scalar.activation(out=own[:], in_=ow[:], func=COPY, scale=edge_weight[:, e : e + 1])
+            return own, gated
+
+        def edge_tile_back(own, gated, dest):
+            turned = psum.tile([P, ROW_TILES, P], F32, name="turned")
+            for r in range(ROW_TILES):
+                cols = slice(r * P, (r + 1) * P)
+                nc.tensor.matmul(turned[:, r, :], own[:, cols], ident[:], start=True, stop=False, is_transpose=True)
+                nc.tensor.matmul(turned[:, r, :], gated[:, cols], ident[:], start=False, stop=True, is_transpose=True)
+            nc.scalar.copy(out=dest, in_=turned[:])
+
+        result = keep.tile([P, ROW_TILES, J], F32, name="result")
+
+        def scatter(r, lo, hi):
+            nc.vector.tensor_copy(
+                pages[r][:].indirect(dst_list[:, lo * P // PER_COLUMN : hi * P // PER_COLUMN]),
+                result[:, r, lo * P : hi * P],
+            )
+            if hi == EDGE_TILES:
+                nc.sync.dma_start(out=out[r * P : (r + 1) * P, :], in_=pages[r][:])
+
+        fronts = {}
+        for step in range(EDGE_TILES + 2):
+            if step < EDGE_TILES:
+                fronts[step] = edge_tile_front(step)
+            if 1 <= step <= EDGE_TILES:
+                e = step - 1
+                edge_tile_back(*fronts[e], result[:, :, e * P : (e + 1) * P])
+            for r in range(ROW_TILES):
+                for lo, hi in zip(SCATTER_CUTS[r], SCATTER_CUTS[r][1:]):
+                    if hi == step - 1:
+                        scatter(r, lo, hi)

@@ -22,13 +22,22 @@ PACK = 4
 PER_COLUMN = 16
 EDGE_TILES = J // P
 ROW_TILES = N // P
-GATHER_CUTS = (0, 256, 512, 1024)
 SCATTER_CUTS = ((0, 2, 6, 8), (0, 3, 6, 8), (0, 4, 8), (0, 5, 8))
 
+BIG = 4 * T
+SMALL = 4 * N
+AT_WA = 0
+AT_WO = BIG
+AT_TABLE = 2 * BIG
+AT_PACKED = 3 * BIG
+AT_LATE = 3 * BIG + 3 * SMALL
+AT_LAST_PAGE = 3 * BIG + 5 * SMALL
+STRADDLE = 2 * P
 
-def load_scale_rows(queue, plane, scales):
+
+def load_scale_rows(nc, plane, scales):
     for q in range(4):
-        queue.dma_start(
+        nc.sync.dma_start(
             out=plane[32 * q : 32 * q + 4, :].bitcast(I32),
             in_=scales[0, 4 * q : 4 * q + 4, :].bitcast(I32),
         )
@@ -44,59 +53,70 @@ def tile_list_rgg_own_kernel(
     nc = tc.nc
     with ExitStack() as ctx:
         keep = ctx.enter_context(tc.tile_pool(name="keep", bufs=1))
-        landing = ctx.enter_context(tc.tile_pool(name="landing", bufs=1))
+        shared = ctx.enter_context(tc.tile_pool(name="shared", bufs=1))
         ring = ctx.enter_context(tc.tile_pool(name="ring", bufs=3))
         psum = ctx.enter_context(tc.psum_pool(name="psum", bufs=2))
 
-        src_list = keep.tile([P, J // PER_COLUMN], U16, name="src_list")
-        dst_list = keep.tile([P, J // PER_COLUMN], U16, name="dst_list")
-        nc.sync.dma_start(dst_list[:], offs2)
-        nc.sync.dma_start(src_list[:], offs)
+        def placed(shape, dtype, name, offset):
+            return shared.tile(shape, dtype, name=name, offset=offset, align_bytes=64)
+
+        lists = {}
+        for side, source in (("dst", offs2), ("src", offs)):
+            lists[side] = keep.tile([P, J // PER_COLUMN], U16, name=side + "_list")
+            nc.sync.dma_start(lists[side][:], source)
 
         tab_plane = keep.tile([P, T], U8, name="tab_plane", align_bytes=64)
         nc.gpsimd.memset(tab_plane[:].bitcast(I32), 0)
-        load_scale_rows(nc.sync, tab_plane, tab_scales)
+        load_scale_rows(nc, tab_plane, tab_scales)
 
-        edge_rows = keep.tile([P, P], F32, name="edge_rows")
+        edge_rows = placed([P, P], F32, "edge_rows", AT_PACKED - STRADDLE)
         nc.vector.memset(edge_rows[:], 0.0)
         nc.sync.dma_start(out=edge_rows[0:EDGE_TILES, :], in_=wgo[0].rearrange("(c m) -> c m", m=P))
 
-        draft = landing.tile([P, 7168], F32, name="draft", offset=0, align_bytes=64)
-        make_identity(nc, draft[:, 0:P])
+        draft = placed([P, P], F32, "draft", AT_WO - STRADDLE)
+        make_identity(nc, draft[:])
         ident = keep.tile([P, P], F32, name="ident")
-        nc.gpsimd.tensor_copy(ident[:], draft[:, 0:P])
+        nc.gpsimd.tensor_copy(ident[:], draft[:])
 
-        planes = {}
-        for name in ("wb", "wc"):
-            planes[name] = keep.tile([P, N], U8, name=name + "_plane", align_bytes=64)
-            nc.gpsimd.memset(planes[name][:].bitcast(I32), 0)
-        load_scale_rows(nc.gpsimd, planes["wc"], wc_scales)
+        warm = keep.tile([P, 8], F32, name="warm")
+        nc.scalar.activation(out=warm[:], in_=ident[:, 0:8], func=SIGMOID)
+
+        wb_plane = keep.tile([P, N], U8, name="wb_plane", align_bytes=64)
+        nc.gpsimd.memset(wb_plane[:].bitcast(I32), 0)
 
         raw = {}
-        for name, w, at in (("wa", wa, 0), ("wo", wo, 8192)):
-            raw[name] = landing.tile([P, PACK, N], F32, name=name + "_raw", offset=at, align_bytes=64)
+        for name, w, offset in (("wa", wa, AT_WA), ("wo", wo, AT_WO)):
+            raw[name] = placed([P, PACK, N], F32, name + "_raw", offset)
             nc.sync.dma_start(out=raw[name][:], in_=w.rearrange("(p i) n -> p i n", i=PACK))
+        load_scale_rows(nc, wb_plane, wb_scales)
 
-        table = landing.tile([P, T], I32, name="table", offset=16384, align_bytes=64)
+        turned = psum.tile([P, ROW_TILES, P], F32, name="turned")
+        nc.tensor.transpose(turned[:, 0, :], edge_rows[:], ident[:])
+        edge_weight = keep.tile([P, EDGE_TILES], F32, name="edge_weight")
+        nc.scalar.copy(out=edge_weight[:], in_=turned[:, 0, 0:EDGE_TILES])
+
+        packed = placed([P, 2 * SMALL + N], U8, "packed", AT_PACKED)
+        codes = {"wb": packed[:, 0:SMALL], "wc": packed[:, SMALL : 2 * SMALL]}
+        planes = {"wb": wb_plane[:], "wc": packed[:, 2 * SMALL :]}
+        nc.sync.dma_start(out=codes["wb"].bitcast(I32), in_=words_of(wb_words))
+        nc.sync.dma_start(out=codes["wc"].bitcast(I32), in_=words_of(wc_words))
+        table = placed([P, T], I32, "table", AT_TABLE)
         nc.sync.dma_start(out=table[:], in_=words_of(tab_words))
-        load_scale_rows(nc.sync, planes["wb"], wb_scales)
-        codes = {}
-        for name, packed, at in (("wb", wb_words, 24576), ("wc", wc_words, 26624)):
-            codes[name] = landing.tile([P, N], I32, name=name + "_codes", offset=at, align_bytes=64)
-            nc.sync.dma_start(out=codes[name][:], in_=words_of(packed))
+        nc.gpsimd.memset(planes["wc"].bitcast(I32), 0)
+        load_scale_rows(nc, planes["wc"], wc_scales)
 
-        pages = [keep.tile([P, T], F32, name="page%d" % r) for r in range(ROW_TILES)]
-        for r in range(2):
-            nc.vector.memset(pages[r][:], 0.0)
+        pages = [keep.tile([P, T], F32, name="page%d" % r) for r in range(2)]
+        for page in pages:
+            nc.vector.memset(page[:], 0.0)
 
-        for r in range(2, ROW_TILES):
-            for half in range(2):
-                nc.gpsimd.memset(pages[r][:, half * J : (half + 1) * J], 0.0)
+        def add_page(offset, engine):
+            pages.append(placed([P, T], F32, "page%d" % len(pages), offset))
+            engine.memset(pages[-1][:], 0.0)
 
         picked_scales = {}
-        for name, lst in (("dst", dst_list), ("src", src_list)):
-            picked_scales[name] = keep.tile([P, J], U8, name=name + "_scales", align_bytes=64)
-            nc.vector.tensor_copy(picked_scales[name][:], tab_plane[:].indirect(lst[:]))
+        for side in ("dst", "src"):
+            picked_scales[side] = keep.tile([P, J], U8, name=side + "_scales", align_bytes=64)
+            nc.vector.tensor_copy(picked_scales[side][:], tab_plane[:].indirect(lists[side][:]))
 
         def quantise(name):
             grouped = keep.tile([P, N, PACK], BF16, name=name + "_grouped", align_bytes=64)
@@ -104,49 +124,48 @@ def tile_list_rgg_own_kernel(
                 out=grouped[:].rearrange("p (c m) i -> p c i m", m=4),
                 in_=raw[name][:].rearrange("p i (c m) -> p c i m", m=4),
             )
-            codes[name] = keep.tile([P, N], U32, name=name + "_codes", align_bytes=64)
-            planes[name] = keep.tile([P, N], U8, name=name + "_plane", align_bytes=64)
+            words = keep.tile([P, N], U32, name=name + "_codes", align_bytes=64)
+            plane = keep.tile([P, N], U8, name=name + "_plane", align_bytes=64)
             nc.vector.quantize_mx(
-                out=codes[name][:].bitcast(FP8X4),
-                scales=planes[name][:],
+                out=words[:].bitcast(FP8X4),
+                scales=plane[:],
                 in_=grouped[:].rearrange("p n i -> p (n i)"),
             )
+            codes[name], planes[name] = words[:], plane[:]
 
         picked_words = {}
 
-        def gather_words(g):
-            lo, hi = GATHER_CUTS[g], GATHER_CUTS[g + 1]
-            for name, lst in (("dst", dst_list), ("src", src_list)):
-                words = keep.tile([P, hi - lo], U32, name="%s_words%d" % (name, g), align_bytes=64)
-                nc.vector.tensor_copy(
-                    words[:], table[:].bitcast(U32).indirect(lst[:, lo // PER_COLUMN : hi // PER_COLUMN])
-                )
-                for e in range(lo // P, hi // P):
-                    picked_words[name, e] = words[:, e * P - lo : (e + 1) * P - lo]
+        def gather_words(side, lo, hi, words):
+            columns = slice(lo * P // PER_COLUMN, hi * P // PER_COLUMN)
+            nc.vector.tensor_copy(words[:], table[:].bitcast(U32).indirect(lists[side][:, columns]))
+            for e in range(lo, hi):
+                picked_words[side, e] = words[:, (e - lo) * P : (e - lo + 1) * P]
+
+        def gather_early(lo, hi):
+            for side in ("dst", "src"):
+                words = keep.tile([P, (hi - lo) * P], U32, name="%s_words%d" % (side, lo), align_bytes=64)
+                gather_words(side, lo, hi, words)
 
         quantise("wa")
-        gather_words(0)
+        add_page(AT_WA, nc.vector)
         quantise("wo")
-        for g in range(1, len(GATHER_CUTS) - 1):
-            gather_words(g)
-
-        turned = psum.tile([P, ROW_TILES, P], F32, name="turned")
-        nc.tensor.transpose(turned[:, 0, :], edge_rows[:], ident[:])
-        edge_weight = keep.tile([P, EDGE_TILES], F32, name="edge_weight")
-        nc.scalar.copy(out=edge_weight[:], in_=turned[:, 0, 0:EDGE_TILES])
+        gather_early(0, 2)
+        gather_early(2, 4)
 
         def product(acc, side, e, weight, start, stop):
             nc.tensor.matmul_mx(
                 out=acc[:],
                 lhsT=picked_words[side, e].bitcast(FP8X4),
                 lhsT_scale=picked_scales[side][:, e * P : (e + 1) * P],
-                rhs=codes[weight][:].bitcast(FP8X4),
-                rhs_scale=planes[weight][:],
+                rhs=codes[weight].bitcast(FP8X4),
+                rhs_scale=planes[weight],
                 start=start,
                 stop=stop,
             )
 
-        def edge_tile_front(e):
+        fronts = {}
+
+        def front(e, eta):
             za = psum.tile([P, N], F32, name="za")
             ms = psum.tile([P, N], F32, name="ms")
             ow = psum.tile([P, N], F32, name="ow")
@@ -154,42 +173,47 @@ def tile_list_rgg_own_kernel(
             product(za, "src", e, "wb", False, True)
             product(ms, "src", e, "wc", True, True)
             product(ow, "dst", e, "wo", True, True)
-            eta = ring.tile([P, N], F32, name="eta")
+            weight = edge_weight[:, e : e + 1]
             nc.scalar.activation(out=eta[:], in_=za[:], func=SIGMOID)
             gated = ring.tile([P, N], F32, name="gated")
-            msg = ring.tile([P, N], F32, name="msg")
-            nc.scalar.activation(out=msg[:], in_=ms[:], func=COPY, scale=edge_weight[:, e : e + 1])
-            nc.gpsimd.tensor_tensor(out=gated[:], in0=msg[:], in1=eta[:], op=MULT)
+            nc.vector.scalar_tensor_tensor(out=gated[:], in0=ms[:], scalar=weight, in1=eta[:], op0=MULT, op1=MULT)
             own = ring.tile([P, N], F32, name="own")
-            nc.scalar.activation(out=own[:], in_=ow[:], func=COPY, scale=edge_weight[:, e : e + 1])
-            return own, gated
-
-        def edge_tile_back(own, gated, dest):
-            turned = psum.tile([P, ROW_TILES, P], F32, name="turned")
-            for r in range(ROW_TILES):
-                cols = slice(r * P, (r + 1) * P)
-                nc.tensor.matmul(turned[:, r, :], own[:, cols], ident[:], start=True, stop=False, is_transpose=True)
-                nc.tensor.matmul(turned[:, r, :], gated[:, cols], ident[:], start=False, stop=True, is_transpose=True)
-            nc.scalar.copy(out=dest, in_=turned[:])
+            nc.scalar.activation(out=own[:], in_=ow[:], func=COPY, scale=weight)
+            fronts[e] = own, gated
 
         result = keep.tile([P, ROW_TILES, J], F32, name="result")
 
-        def scatter(r, lo, hi):
-            nc.vector.tensor_copy(
-                pages[r][:].indirect(dst_list[:, lo * P // PER_COLUMN : hi * P // PER_COLUMN]),
-                result[:, r, lo * P : hi * P],
-            )
-            if hi == EDGE_TILES:
-                nc.sync.dma_start(out=out[r * P : (r + 1) * P, :], in_=pages[r][:])
-
-        fronts = {}
-        for step in range(EDGE_TILES + 2):
-            if step < EDGE_TILES:
-                fronts[step] = edge_tile_front(step)
-            if 1 <= step <= EDGE_TILES:
-                e = step - 1
-                edge_tile_back(*fronts[e], result[:, :, e * P : (e + 1) * P])
+        def back(e):
+            own, gated = fronts[e]
+            turned = psum.tile([P, ROW_TILES, P], F32, name="turned")
+            for r in range(ROW_TILES):
+                rows = slice(r * P, (r + 1) * P)
+                nc.tensor.matmul(turned[:, r, :], own[:, rows], ident[:], start=True, stop=False, is_transpose=True)
+                nc.tensor.matmul(turned[:, r, :], gated[:, rows], ident[:], start=False, stop=True, is_transpose=True)
+            nc.scalar.copy(out=result[:, :, e * P : (e + 1) * P], in_=turned[:])
             for r in range(ROW_TILES):
                 for lo, hi in zip(SCATTER_CUTS[r], SCATTER_CUTS[r][1:]):
-                    if hi == step - 1:
-                        scatter(r, lo, hi)
+                    if hi == e + 1:
+                        columns = slice(lo * P // PER_COLUMN, hi * P // PER_COLUMN)
+                        nc.vector.tensor_copy(
+                            pages[r][:].indirect(lists["dst"][:, columns]), result[:, r, lo * P : hi * P]
+                        )
+                        if hi == EDGE_TILES:
+                            nc.sync.dma_start(out=out[r * P : (r + 1) * P, :], in_=pages[r][:])
+
+        half = EDGE_TILES // 2
+        front(0, placed([P, N], F32, "eta0", AT_LATE))
+        gather_words("dst", half, EDGE_TILES, placed([P, N], U32, "dst_late", AT_LATE))
+        front(1, placed([P, N], F32, "eta1", AT_LATE + SMALL))
+        gather_words("src", half, EDGE_TILES, placed([P, N], U32, "src_late", AT_LATE + SMALL))
+        back(0)
+        front(2, placed([P, N], F32, "eta2", AT_LAST_PAGE))
+        add_page(AT_LAST_PAGE, nc.vector)
+        back(1)
+        for e in range(3, EDGE_TILES - 1):
+            front(e, ring.tile([P, N], F32, name="eta"))
+            if e < EDGE_TILES - 2:
+                back(e - 1)
+        front(EDGE_TILES - 1, ring.tile([P, N], F32, name="eta"))
+        for e in range(EDGE_TILES - 3, EDGE_TILES):
+            back(e)

@@ -22,22 +22,19 @@ PACK = 4
 PER_COLUMN = 16
 EDGE_TILES = J // P
 ROW_TILES = N // P
-SCATTER_CUTS = ((0, 2, 6, 8), (0, 3, 6, 8), (0, 4, 8), (0, 5, 8))
+SCATTER_CUTS = ((0, 2, 4, 6, 8), (0, 2, 4, 6, 8), (0, 2, 5, 8), (0, 3, 5, 8))
 
 BIG = 4 * T
 SMALL = 4 * N
-AT_WA = 0
-AT_WO = BIG
-AT_TABLE = 2 * BIG
-AT_PACKED = 3 * BIG
-AT_LATE = 3 * BIG + 3 * SMALL
-AT_LAST_PAGE = 3 * BIG + 5 * SMALL
-STRADDLE = 2 * P
+AT_WO = 0
+AT_TABLE = BIG
+AT_PACKED = 2 * BIG
+AT_LATE = 2 * BIG + 2 * SMALL
 
 
-def load_scale_rows(nc, plane, scales):
+def load_scale_rows(queue, plane, scales):
     for q in range(4):
-        nc.sync.dma_start(
+        queue.dma_start(
             out=plane[32 * q : 32 * q + 4, :].bitcast(I32),
             in_=scales[0, 4 * q : 4 * q + 4, :].bitcast(I32),
         )
@@ -65,58 +62,63 @@ def tile_list_rgg_own_kernel(
             lists[side] = keep.tile([P, J // PER_COLUMN], U16, name=side + "_list")
             nc.sync.dma_start(lists[side][:], source)
 
+        warm_in = placed([P, 32], F32, "warm_in", AT_TABLE - 64)
+        warm_out = placed([P, 32], F32, "warm_out", AT_PACKED)
+        nc.gpsimd.memset(warm_in[:], 0.0)
+        nc.scalar.activation(out=warm_out[:], in_=warm_in[:], func=SIGMOID)
+
         tab_plane = keep.tile([P, T], U8, name="tab_plane", align_bytes=64)
         nc.gpsimd.memset(tab_plane[:].bitcast(I32), 0)
-        load_scale_rows(nc, tab_plane, tab_scales)
+        load_scale_rows(nc.sync, tab_plane, tab_scales)
 
-        edge_rows = placed([P, P], F32, "edge_rows", AT_PACKED - STRADDLE)
-        nc.vector.memset(edge_rows[:], 0.0)
-        nc.sync.dma_start(out=edge_rows[0:EDGE_TILES, :], in_=wgo[0].rearrange("(c m) -> c m", m=P))
+        raw = {"wa": keep.tile([P, PACK, N], F32, name="wa_raw")}
+        nc.sync.dma_start(out=raw["wa"][:], in_=wa.rearrange("(p i) n -> p i n", i=PACK))
 
-        draft = placed([P, P], F32, "draft", AT_WO - STRADDLE)
-        make_identity(nc, draft[:])
+        table = placed([P, T], I32, "table", AT_TABLE)
+        nc.sync.dma_start(out=table[:], in_=words_of(tab_words))
+        raw["wo"] = placed([P, PACK, N], F32, "wo_raw", AT_WO)
+        nc.sync.dma_start(out=raw["wo"][:], in_=wo.rearrange("(p i) n -> p i n", i=PACK))
+        packed = placed([P, 2 * N], I32, "packed", AT_PACKED)
+        codes = {"wb": packed[:, 0:N], "wc": packed[:, N:]}
+        nc.sync.dma_start(out=codes["wb"], in_=words_of(wb_words))
+        nc.sync.dma_start(out=codes["wc"], in_=words_of(wc_words))
+
+        pages = [keep.tile([P, T], F32, name="page%d" % r) for r in range(ROW_TILES)]
+        for page in pages[:2]:
+            nc.vector.memset(page[:], 0.0)
+
+        edge_rows = keep.tile([P, P], F32, name="edge_rows")
+        nc.gpsimd.memset(edge_rows[:], 0.0)
+        nc.gpsimd.dma_start(out=edge_rows[0:EDGE_TILES, :], in_=wgo[0].rearrange("(c m) -> c m", m=P))
+        planes = {}
+        for name, scales, clears, loads in (("wb", wb_scales, nc.vector, nc.sync), ("wc", wc_scales, nc.gpsimd, nc.gpsimd)):
+            plane = keep.tile([P, N], U8, name=name + "_plane", align_bytes=64)
+            clears.memset(plane[:].bitcast(I32), 0)
+            load_scale_rows(loads, plane, scales)
+            planes[name] = plane[:]
         ident = keep.tile([P, P], F32, name="ident")
-        nc.gpsimd.tensor_copy(ident[:], draft[:])
-
-        warm = keep.tile([P, 8], F32, name="warm")
-        nc.scalar.activation(out=warm[:], in_=ident[:, 0:8], func=SIGMOID)
-
-        wb_plane = keep.tile([P, N], U8, name="wb_plane", align_bytes=64)
-        nc.gpsimd.memset(wb_plane[:].bitcast(I32), 0)
-
-        raw = {}
-        for name, w, offset in (("wa", wa, AT_WA), ("wo", wo, AT_WO)):
-            raw[name] = placed([P, PACK, N], F32, name + "_raw", offset)
-            nc.sync.dma_start(out=raw[name][:], in_=w.rearrange("(p i) n -> p i n", i=PACK))
-        load_scale_rows(nc, wb_plane, wb_scales)
+        make_identity(nc, ident[:])
 
         turned = psum.tile([P, ROW_TILES, P], F32, name="turned")
         nc.tensor.transpose(turned[:, 0, :], edge_rows[:], ident[:])
         edge_weight = keep.tile([P, EDGE_TILES], F32, name="edge_weight")
         nc.scalar.copy(out=edge_weight[:], in_=turned[:, 0, 0:EDGE_TILES])
 
-        packed = placed([P, 2 * SMALL + N], U8, "packed", AT_PACKED)
-        codes = {"wb": packed[:, 0:SMALL], "wc": packed[:, SMALL : 2 * SMALL]}
-        planes = {"wb": wb_plane[:], "wc": packed[:, 2 * SMALL :]}
-        nc.sync.dma_start(out=codes["wb"].bitcast(I32), in_=words_of(wb_words))
-        nc.sync.dma_start(out=codes["wc"].bitcast(I32), in_=words_of(wc_words))
-        table = placed([P, T], I32, "table", AT_TABLE)
-        nc.sync.dma_start(out=table[:], in_=words_of(tab_words))
-        nc.gpsimd.memset(planes["wc"].bitcast(I32), 0)
-        load_scale_rows(nc, planes["wc"], wc_scales)
-
-        pages = [keep.tile([P, T], F32, name="page%d" % r) for r in range(2)]
-        for page in pages:
-            nc.vector.memset(page[:], 0.0)
-
-        def add_page(offset, engine):
-            pages.append(placed([P, T], F32, "page%d" % len(pages), offset))
-            engine.memset(pages[-1][:], 0.0)
+        for page in pages[2:]:
+            for half in range(2):
+                nc.gpsimd.memset(page[:, half * J : (half + 1) * J], 0.0)
 
         picked_scales = {}
-        for side in ("dst", "src"):
-            picked_scales[side] = keep.tile([P, J], U8, name=side + "_scales", align_bytes=64)
-            nc.vector.tensor_copy(picked_scales[side][:], tab_plane[:].indirect(lists[side][:]))
+
+        def gather_scales(side, lo, hi, picked):
+            columns = slice(lo * P // PER_COLUMN, hi * P // PER_COLUMN)
+            nc.vector.tensor_copy(picked[:], tab_plane[:].indirect(lists[side][:, columns]))
+            for e in range(lo, hi):
+                picked_scales[side, e] = picked[:, (e - lo) * P : (e - lo + 1) * P]
+
+        half = EDGE_TILES // 2
+        gather_scales("dst", 0, EDGE_TILES, keep.tile([P, J], U8, name="dst_scales", align_bytes=64))
+        gather_scales("src", 0, half, keep.tile([P, half * P], U8, name="src_scales", align_bytes=64))
 
         def quantise(name):
             grouped = keep.tile([P, N, PACK], BF16, name=name + "_grouped", align_bytes=64)
@@ -147,16 +149,15 @@ def tile_list_rgg_own_kernel(
                 gather_words(side, lo, hi, words)
 
         quantise("wa")
-        add_page(AT_WA, nc.vector)
-        quantise("wo")
         gather_early(0, 2)
+        quantise("wo")
         gather_early(2, 4)
 
         def product(acc, side, e, weight, start, stop):
             nc.tensor.matmul_mx(
                 out=acc[:],
                 lhsT=picked_words[side, e].bitcast(FP8X4),
-                lhsT_scale=picked_scales[side][:, e * P : (e + 1) * P],
+                lhsT_scale=picked_scales[side, e],
                 rhs=codes[weight].bitcast(FP8X4),
                 rhs_scale=planes[weight],
                 start=start,
@@ -176,7 +177,12 @@ def tile_list_rgg_own_kernel(
             weight = edge_weight[:, e : e + 1]
             nc.scalar.activation(out=eta[:], in_=za[:], func=SIGMOID)
             gated = ring.tile([P, N], F32, name="gated")
-            nc.vector.scalar_tensor_tensor(out=gated[:], in0=ms[:], scalar=weight, in1=eta[:], op0=MULT, op1=MULT)
+            if e < 2:
+                nc.vector.scalar_tensor_tensor(out=gated[:], in0=ms[:], scalar=weight, in1=eta[:], op0=MULT, op1=MULT)
+            else:
+                msg = ring.tile([P, N], F32, name="msg")
+                nc.scalar.activation(out=msg[:], in_=ms[:], func=COPY, scale=weight)
+                nc.gpsimd.tensor_tensor(out=gated[:], in0=msg[:], in1=eta[:], op=MULT)
             own = ring.tile([P, N], F32, name="own")
             nc.scalar.activation(out=own[:], in_=ow[:], func=COPY, scale=weight)
             fronts[e] = own, gated
@@ -201,19 +207,15 @@ def tile_list_rgg_own_kernel(
                         if hi == EDGE_TILES:
                             nc.sync.dma_start(out=out[r * P : (r + 1) * P, :], in_=pages[r][:])
 
-        half = EDGE_TILES // 2
-        front(0, placed([P, N], F32, "eta0", AT_LATE))
+        front(0, ring.tile([P, N], F32, name="eta"))
+        front(1, placed([P, N], F32, "eta1", AT_LATE + SMALL // 2))
         gather_words("dst", half, EDGE_TILES, placed([P, N], U32, "dst_late", AT_LATE))
-        front(1, placed([P, N], F32, "eta1", AT_LATE + SMALL))
-        gather_words("src", half, EDGE_TILES, placed([P, N], U32, "src_late", AT_LATE + SMALL))
+        gather_scales("src", half, EDGE_TILES, placed([P, half * P], U8, "src_late_scales", AT_LATE + SMALL))
+        gather_words("src", half, EDGE_TILES, placed([P, N], U32, "src_late", AT_LATE + SMALL + half * P))
         back(0)
-        front(2, placed([P, N], F32, "eta2", AT_LAST_PAGE))
-        add_page(AT_LAST_PAGE, nc.vector)
         back(1)
-        for e in range(3, EDGE_TILES - 1):
+        for e in range(2, EDGE_TILES):
             front(e, ring.tile([P, N], F32, name="eta"))
-            if e < EDGE_TILES - 2:
+            if e >= 3:
                 back(e - 1)
-        front(EDGE_TILES - 1, ring.tile([P, N], F32, name="eta"))
-        for e in range(EDGE_TILES - 3, EDGE_TILES):
-            back(e)
+        back(EDGE_TILES - 1)

@@ -83,7 +83,7 @@ def tile_list_rgg_own_kernel(
         nc.sync.dma_start(out=codes["wb"], in_=words_of(wb_words))
         nc.sync.dma_start(out=codes["wc"], in_=words_of(wc_words))
 
-        pages = [keep.tile([P, T], F32, name="page%d" % r) for r in range(ROW_TILES)]
+        pages = [keep.tile([P, T], F32, name="page%d" % r) for r in range(ROW_TILES - 1)]
         for page in pages[:2]:
             nc.vector.memset(page[:], 0.0)
 
@@ -104,9 +104,7 @@ def tile_list_rgg_own_kernel(
         edge_weight = keep.tile([P, EDGE_TILES], F32, name="edge_weight")
         nc.scalar.copy(out=edge_weight[:], in_=turned[:, 0, 0:EDGE_TILES])
 
-        for page in pages[2:]:
-            for half in range(2):
-                nc.gpsimd.memset(page[:, half * J : (half + 1) * J], 0.0)
+        nc.vector.memset(pages[2][:], 0.0)
 
         picked_scales = {}
 
@@ -152,6 +150,8 @@ def tile_list_rgg_own_kernel(
         gather_early(0, 2)
         quantise("wo")
         gather_early(2, 4)
+        pages.append(placed([P, T], F32, "page3", AT_WO))
+        nc.vector.memset(pages[3][:], 0.0)
 
         def product(acc, side, e, weight, start, stop):
             nc.tensor.matmul_mx(

from contextlib import ExitStack

import concourse.mybir as mybir
from concourse.masks import make_identity

K, N, T, J = 512, 512, 2048, 1024
FLOPS = 4 * 2 * K * N * J

F32 = mybir.dt.float32
BF16 = mybir.dt.bfloat16
I32 = mybir.dt.int32
U32 = mybir.dt.uint32
U16 = mybir.dt.uint16
U8 = mybir.dt.uint8
FP8X4 = mybir.dt.float8_e4m3fn_x4
MULT = mybir.AluOpType.mult
SIGMOID = mybir.ActivationFunctionType.Sigmoid
COPY = mybir.ActivationFunctionType.Copy

P = 128
PACK = 4
PER_COLUMN = 16
EDGE_TILES = J // P
ROW_TILES = N // P
SCATTER_CUTS = ((0, 2, 4, 6, 8), (0, 2, 4, 6, 8), (0, 2, 5, 8), (0, 3, 5, 8))

BIG = 4 * T
SMALL = 4 * N
AT_WO = 0
AT_TABLE = BIG
AT_PACKED = 2 * BIG
AT_LATE = 2 * BIG + 2 * SMALL


def load_scale_rows(queue, plane, scales):
    for q in range(4):
        queue.dma_start(
            out=plane[32 * q : 32 * q + 4, :].bitcast(I32),
            in_=scales[0, 4 * q : 4 * q + 4, :].bitcast(I32),
        )


def words_of(packed):
    return packed[0].rearrange("p c i -> p (c i)").bitcast(I32)


def tile_list_rgg_own_kernel(
    tc, tab_words, tab_scales, wa, wb_words, wb_scales, wc_words, wc_scales, wo, wgo, offs, offs2, out
):
    nc = tc.nc
    with ExitStack() as ctx:
        keep = ctx.enter_context(tc.tile_pool(name="keep", bufs=1))
        shared = ctx.enter_context(tc.tile_pool(name="shared", bufs=1))
        ring = ctx.enter_context(tc.tile_pool(name="ring", bufs=3))
        psum = ctx.enter_context(tc.psum_pool(name="psum", bufs=2))

        def placed(shape, dtype, name, offset):
            return shared.tile(shape, dtype, name=name, offset=offset, align_bytes=64)

        lists = {}
        for side, source in (("dst", offs2), ("src", offs)):
            lists[side] = keep.tile([P, J // PER_COLUMN], U16, name=side + "_list")
            nc.sync.dma_start(lists[side][:], source)

        warm_in = placed([P, 32], F32, "warm_in", AT_TABLE - 64)
        warm_out = placed([P, 32], F32, "warm_out", AT_PACKED)
        nc.gpsimd.memset(warm_in[:], 0.0)
        nc.scalar.activation(out=warm_out[:], in_=warm_in[:], func=SIGMOID)

        tab_plane = keep.tile([P, T], U8, name="tab_plane", align_bytes=64)
        nc.gpsimd.memset(tab_plane[:].bitcast(I32), 0)
        load_scale_rows(nc.sync, tab_plane, tab_scales)

        raw = {"wa": keep.tile([P, PACK, N], F32, name="wa_raw")}
        nc.sync.dma_start(out=raw["wa"][:], in_=wa.rearrange("(p i) n -> p i n", i=PACK))

        table = placed([P, T], I32, "table", AT_TABLE)
        nc.sync.dma_start(out=table[:], in_=words_of(tab_words))
        raw["wo"] = placed([P, PACK, N], F32, "wo_raw", AT_WO)
        nc.sync.dma_start(out=raw["wo"][:], in_=wo.rearrange("(p i) n -> p i n", i=PACK))
        packed = placed([P, 2 * N], I32, "packed", AT_PACKED)
        codes = {"wb": packed[:, 0:N], "wc": packed[:, N:]}
        nc.sync.dma_start(out=codes["wb"], in_=words_of(wb_words))
        nc.sync.dma_start(out=codes["wc"], in_=words_of(wc_words))

        pages = [keep.tile([P, T], F32, name="page%d" % r) for r in range(ROW_TILES - 1)]
        for page in pages[:2]:
            nc.vector.memset(page[:], 0.0)

        edge_rows = keep.tile([P, P], F32, name="edge_rows")
        nc.gpsimd.memset(edge_rows[:], 0.0)
        nc.gpsimd.dma_start(out=edge_rows[0:EDGE_TILES, :], in_=wgo[0].rearrange("(c m) -> c m", m=P))
        planes = {}
        for name, scales, clears, loads in (("wb", wb_scales, nc.vector, nc.sync), ("wc", wc_scales, nc.gpsimd, nc.gpsimd)):
            plane = keep.tile([P, N], U8, name=name + "_plane", align_bytes=64)
            clears.memset(plane[:].bitcast(I32), 0)
            load_scale_rows(loads, plane, scales)
            planes[name] = plane[:]
        ident = keep.tile([P, P], F32, name="ident")
        make_identity(nc, ident[:])

        turned = psum.tile([P, ROW_TILES, P], F32, name="turned")
        nc.tensor.transpose(turned[:, 0, :], edge_rows[:], ident[:])
        edge_weight = keep.tile([P, EDGE_TILES], F32, name="edge_weight")
        nc.scalar.copy(out=edge_weight[:], in_=turned[:, 0, 0:EDGE_TILES])

        nc.vector.memset(pages[2][:], 0.0)

        picked_scales = {}

        def gather_scales(side, lo, hi, picked):
            columns = slice(lo * P // PER_COLUMN, hi * P // PER_COLUMN)
            nc.vector.tensor_copy(picked[:], tab_plane[:].indirect(lists[side][:, columns]))
            for e in range(lo, hi):
                picked_scales[side, e] = picked[:, (e - lo) * P : (e - lo + 1) * P]

        half = EDGE_TILES // 2
        gather_scales("dst", 0, EDGE_TILES, keep.tile([P, J], U8, name="dst_scales", align_bytes=64))
        gather_scales("src", 0, half, keep.tile([P, half * P], U8, name="src_scales", align_bytes=64))

        def quantise(name):
            grouped = keep.tile([P, N, PACK], BF16, name=name + "_grouped", align_bytes=64)
            nc.scalar.copy(
                out=grouped[:].rearrange("p (c m) i -> p c i m", m=4),
                in_=raw[name][:].rearrange("p i (c m) -> p c i m", m=4),
            )
            words = keep.tile([P, N], U32, name=name + "_codes", align_bytes=64)
            plane = keep.tile([P, N], U8, name=name + "_plane", align_bytes=64)
            nc.vector.quantize_mx(
                out=words[:].bitcast(FP8X4),
                scales=plane[:],
                in_=grouped[:].rearrange("p n i -> p (n i)"),
            )
            codes[name], planes[name] = words[:], plane[:]

        picked_words = {}

        def gather_words(side, lo, hi, words):
            columns = slice(lo * P // PER_COLUMN, hi * P // PER_COLUMN)
            nc.vector.tensor_copy(words[:], table[:].bitcast(U32).indirect(lists[side][:, columns]))
            for e in range(lo, hi):
                picked_words[side, e] = words[:, (e - lo) * P : (e - lo + 1) * P]

        def gather_early(lo, hi):
            for side in ("dst", "src"):
                words = keep.tile([P, (hi - lo) * P], U32, name="%s_words%d" % (side, lo), align_bytes=64)
                gather_words(side, lo, hi, words)

        quantise("wa")
        gather_early(0, 2)
        quantise("wo")
        gather_early(2, 4)
        pages.append(placed([P, T], F32, "page3", AT_WO))
        nc.vector.memset(pages[3][:], 0.0)

        def product(acc, side, e, weight, start, stop):
            nc.tensor.matmul_mx(
                out=acc[:],
                lhsT=picked_words[side, e].bitcast(FP8X4),
                lhsT_scale=picked_scales[side, e],
                rhs=codes[weight].bitcast(FP8X4),
                rhs_scale=planes[weight],
                start=start,
                stop=stop,
            )

        fronts = {}

        def front(e, eta):
            za = psum.tile([P, N], F32, name="za")
            ms = psum.tile([P, N], F32, name="ms")
            ow = psum.tile([P, N], F32, name="ow")
            product(za, "dst", e, "wa", True, False)
            product(za, "src", e, "wb", False, True)
            product(ms, "src", e, "wc", True, True)
            product(ow, "dst", e, "wo", True, True)
            weight = edge_weight[:, e : e + 1]
            nc.scalar.activation(out=eta[:], in_=za[:], func=SIGMOID)
            gated = ring.tile([P, N], F32, name="gated")
            if e < 2:
                nc.vector.scalar_tensor_tensor(out=gated[:], in0=ms[:], scalar=weight, in1=eta[:], op0=MULT, op1=MULT)
            else:
                msg = ring.tile([P, N], F32, name="msg")
                nc.scalar.activation(out=msg[:], in_=ms[:], func=COPY, scale=weight)
                nc.gpsimd.tensor_tensor(out=gated[:], in0=msg[:], in1=eta[:], op=MULT)
            own = ring.tile([P, N], F32, name="own")
            nc.scalar.activation(out=own[:], in_=ow[:], func=COPY, scale=weight)
            fronts[e] = own, gated

        result = keep.tile([P, ROW_TILES, J], F32, name="result")

        def back(e):
            own, gated = fronts[e]
            turned = psum.tile([P, ROW_TILES, P], F32, name="turned")
            for r in range(ROW_TILES):
                rows = slice(r * P, (r + 1) * P)
                nc.tensor.matmul(turned[:, r, :], own[:, rows], ident[:], start=True, stop=False, is_transpose=True)
                nc.tensor.matmul(turned[:, r, :], gated[:, rows], ident[:], start=False, stop=True, is_transpose=True)
            nc.scalar.copy(out=result[:, :, e * P : (e + 1) * P], in_=turned[:])
            for r in range(ROW_TILES):
                for lo, hi in zip(SCATTER_CUTS[r], SCATTER_CUTS[r][1:]):
                    if hi == e + 1:
                        columns = slice(lo * P // PER_COLUMN, hi * P // PER_COLUMN)
                        nc.vector.tensor_copy(
                            pages[r][:].indirect(lists["dst"][:, columns]), result[:, r, lo * P : hi * P]
                        )
                        if hi == EDGE_TILES:
                            nc.sync.dma_start(out=out[r * P : (r + 1) * P, :], in_=pages[r][:])

        front(0, ring.tile([P, N], F32, name="eta"))
        front(1, placed([P, N], F32, "eta1", AT_LATE + SMALL // 2))
        gather_words("dst", half, EDGE_TILES, placed([P, N], U32, "dst_late", AT_LATE))
        gather_scales("src", half, EDGE_TILES, placed([P, half * P], U8, "src_late_scales", AT_LATE + SMALL))
        gather_words("src", half, EDGE_TILES, placed([P, N], U32, "src_late", AT_LATE + SMALL + half * P))
        back(0)
        back(1)
        for e in range(2, EDGE_TILES):
            front(e, ring.tile([P, N], F32, name="eta"))
            if e >= 3:
                back(e - 1)
        back(EDGE_TILES - 1)
